import numpy as np
import ml_dtypes


def mxq(x, axis, fmt="e4m3"):
    dtype, down = {"e4m3": (ml_dtypes.float8_e4m3fn, 7), "e5m2": (ml_dtypes.float8_e5m2, 14)}[fmt]
    v = np.moveaxis(np.asarray(x, np.float32).astype(ml_dtypes.bfloat16).astype(np.float64), axis, -1)
    blocks = v.reshape(v.shape[:-1] + (-1, 32))
    amax = np.abs(blocks).max(-1, keepdims=True)
    byte = np.maximum(np.where(amax > 0, np.frexp(amax)[1] - 1 + 127, 0) - down, 1)
    scale = np.exp2(byte - 127.0)
    codes = (blocks / scale).astype(np.float32).astype(dtype).astype(np.float64)
    return np.moveaxis((codes * scale).reshape(v.shape), -1, axis)


WIDE = False


def mx_kscale(k):
    if not WIDE:
        return np.ones(k)
    levels = np.array([10, -10, 5, -5, 0])
    if k % 512:
        return np.exp2(np.random.permutation(np.resize(levels, k // 32))).repeat(32)
    a = np.empty((k // 512, 16))
    for p in range(k // 512):
        a[p, :8] = np.random.permutation(np.resize(levels, 8))
        for g in range(8):
            far = levels[np.abs(levels - a[p, g]) >= 10]
            a[p, g + 8] = far[np.random.randint(len(far))]
    return np.exp2(a.ravel()).repeat(32)


def f64(x):
    return np.asarray(x).astype(np.float64)


def striped(idx):
    return np.tile(idx.reshape(-1, 16).T, (8, 1)).astype(np.uint16)


def unstriped(offs):
    return offs[:16].T.reshape(-1).astype(np.int64)


def pack_weight(w):
    k, n = w.shape
    w = f64(np.asarray(w, np.float32).astype(ml_dtypes.bfloat16)).reshape(k // 32, 32, n)
    amax = np.abs(w).max(1)
    byte = np.clip(np.where(amax > 0, np.frexp(amax)[1] - 1 + 127 - 7, 1), 1, 254)
    scaled = (w * np.exp2(127.0 - byte)[:, None, :]).reshape(k, n).astype(np.float32)
    words = np.ascontiguousarray(scaled.reshape(k // 512, 128, 4, n).transpose(0, 1, 3, 2)).astype(ml_dtypes.float8_e4m3fn).view(np.uint8)
    return words, np.ascontiguousarray(byte.astype(np.uint8).reshape(k // 512, 16, n))


def unpack_weight(words, scales):
    g, p, n, _ = words.shape
    vals = np.ascontiguousarray(words).view(ml_dtypes.float8_e4m3fn).astype(np.float64) * np.repeat(np.exp2(scales.astype(np.float64) - 127.0), 8, axis=1)[..., None]
    return vals.transpose(0, 1, 3, 2).reshape(g * 512, n)


E2M1 = np.array([0.0, 0.5, 1.0, 1.5, 2.0, 3.0, 4.0, 6.0, -0.0, -0.5, -1.0, -1.5, -2.0, -3.0, -4.0, -6.0])


def pack_fp4(w):
    k, n = w.shape
    w = f64(np.asarray(w, np.float32).astype(ml_dtypes.bfloat16)).reshape(k // 32, 32, n)
    amax = np.abs(w).max(1)
    mant, ex = np.frexp(amax / 6.0)
    byte = np.clip(np.where(amax > 0, np.where(mant > 0.5, ex, ex - 1) + 127, 1), 1, 254)
    scaled = (w * np.exp2(127.0 - byte)[:, None, :]).reshape(k, n).astype(np.float32)
    c = np.ascontiguousarray(scaled.reshape(k // 512, 128, 4, n).transpose(0, 1, 3, 2)).astype(ml_dtypes.float4_e2m1fn).view(np.uint8) & 0xF
    words = (c[..., 0::2] | (c[..., 1::2] << 4)).reshape(k // 512, 128, 2 * n)
    return np.ascontiguousarray(words), np.ascontiguousarray(byte.astype(np.uint8).reshape(k // 512, 16, n))


def unpack_fp4(words, scales):
    g, _, n = scales.shape
    words = np.ascontiguousarray(words).reshape(g, 128, n, 2)
    nib = np.empty((g, 128, n, 4), np.uint8)
    nib[..., 0::2] = words & 0xF
    nib[..., 1::2] = words >> 4
    vals = E2M1[nib] * np.repeat(np.exp2(scales.astype(np.float64) - 127.0), 8, axis=1)[..., None]
    return vals.transpose(0, 1, 3, 2).reshape(g * 512, n)


K, T, S, D, N, H, V, U = 512, 4096, 1024, 4, 256, 512, 256, 512


def setup_inputs():
    n = np.random.standard_normal
    s = mx_kscale(K)[:, None]
    u = mx_kscale(H)
    packed_xT = pack_weight(n((K, T)) * s)
    packed_w1 = pack_fp4(n((K, H)) / np.sqrt(K) / s)
    packed_w2 = pack_fp4(n((H, N)) / np.sqrt(H) / u[:, None])
    return {
        "x_words": packed_xT[0],
        "x_scales": packed_xT[1],
        "w1_words": packed_w1[0],
        "w1_scales": packed_w1[1],
        "lod": (n((H, U))).astype(np.float32),
        "unit": (np.random.uniform(0.6, 1.4, (H, 1)) * u[:, None]).astype(np.float32),
        "w2_words": packed_w2[0],
        "w2_scales": packed_w2[1],
        "offs": striped(np.random.permutation(T)[:S]),
        "par": striped(np.random.permutation(np.concatenate([np.arange(V), np.random.randint(0, V, U - V)]))),
        "nb": striped(np.random.permutation(U)),
    }


def reference(x_words, x_scales, w1_words, w1_scales, lod, unit, w2_words, w2_scales, offs, par, nb):
    xq = unpack_weight(x_words, x_scales)[:, unstriped(offs)]
    y = unpack_fp4(w1_words, w1_scales).T @ xq
    lev1 = y.reshape(len(y), -1, D).max(axis=2)
    lp = lev1[:, unstriped(par)]
    lev2 = lp + 0.7 * f64(lod)
    smo = 0.5 * (lev2 + lev2[:, unstriped(nb)])
    det = lev2 - smo
    hid = f64(unit) * (smo * (np.exp(0.8 * np.tanh(det))))
    return unpack_fp4(w2_words, w2_scales).T @ mxq(hid, 0, "e4m3")

@@ -1,0 +1,178 @@
+import math
+from contextlib import ExitStack
+
+import concourse.mybir as mybir
+
+K, T, S, D, N, H, V, U = 512, 4096, 1024, 4, 256, 512, 256, 512
+FLOPS = 2 * K * H * S + 2 * H * N * U
+
+F32 = mybir.dt.float32
+BF16 = mybir.dt.bfloat16
+I32 = mybir.dt.int32
+U32 = mybir.dt.uint32
+U16 = mybir.dt.uint16
+U8 = mybir.dt.uint8
+FP8X4 = mybir.dt.float8_e4m3fn_x4
+FP4X4 = mybir.dt.float4_e2m1fn_x4
+ALU = mybir.AluOpType
+ACT = mybir.ActivationFunctionType
+AXIS = mybir.AxisListType
+
+P = 128
+PACK = 4
+HALF = 512
+SCALE_ROWS = 16
+PARK = P - SCALE_ROWS
+LEV1_WINDOW = 704
+CHUNKS = ((0, 256), (256, 512))
+
+
+def tile_picked_yoctree_exp_p_kernel(
+    tc, x_words, x_scales, w1_words, w1_scales, lod, unit, w2_words, w2_scales, offs, par, nb, out
+):
+    nc = tc.nc
+    with ExitStack() as ctx:
+        lists = ctx.enter_context(tc.tile_pool(name="lists", bufs=1))
+        keep = ctx.enter_context(tc.tile_pool(name="keep", bufs=1))
+        psum = ctx.enter_context(tc.psum_pool(name="psum", bufs=1))
+
+        offs_sb = lists.tile([P, S // 16], U16, name="offs_sb")
+        par_sb = lists.tile([P, U // 16], U16, name="par_sb")
+        nb_sb = lists.tile([P, U // 16], U16, name="nb_sb")
+
+        xw = keep.tile([P, T], U32, name="xw", align_bytes=64)
+        xs = keep.tile([P, T], U8, name="xs", align_bytes=64)
+        w1w_raw = keep.tile([P, 2 * H], U8, name="w1w_raw", align_bytes=64)
+        w1s_raw = keep.tile([P, H], U8, name="w1s_raw", align_bytes=64)
+        w1w = keep.tile([P, 2 * H], U8, name="w1w", align_bytes=64)
+        w1s = keep.tile([P, H], U8, name="w1s", align_bytes=64)
+        w2w = keep.tile([P, 2 * N], U8, name="w2w", align_bytes=64)
+        w2s = keep.tile([P, N], U8, name="w2s", align_bytes=64)
+        unit_sb = keep.tile([P, PACK], F32, name="unit_sb")
+        xs_picked = keep.tile([P, S], U8, name="xs_picked", tag="picked_then_lod", align_bytes=64)
+        xs_placed = keep.tile([P, S], U8, name="xs_placed", align_bytes=64)
+
+        nc.sync.dma_start(offs_sb[:], offs)
+        nc.scalar.dma_start(xs[PARK:P, :].bitcast(I32), x_scales[0].bitcast(I32))
+        nc.sync.dma_start(par_sb[:], par)
+        nc.scalar.dma_start(w1w_raw[:].bitcast(I32), w1_words[0].bitcast(I32))
+        nc.sync.dma_start(xw[:].bitcast(I32), x_words[0].rearrange("p n t -> p (n t)").bitcast(I32))
+        nc.sync.dma_start(nb_sb[:], nb)
+
+        nc.vector.memset(xs[0:PARK, :].bitcast(I32), 0)
+        nc.vector.memset(xs_placed[:].bitcast(I32), 0)
+        nc.gpsimd.memset(w1s_raw[:].bitcast(I32), 0)
+        for j in range(4):
+            queue = nc.scalar if j < 2 else nc.gpsimd
+            queue.dma_start(w1s_raw[j:P:32, :].bitcast(I32), w1_scales[0, j:SCALE_ROWS:4, :].bitcast(I32))
+        lev1 = []
+        for t in range(PACK):
+            window = keep.tile([P, LEV1_WINDOW], F32, name="lev1_%d" % t)
+            nc.gpsimd.memset(window[:, V:LEV1_WINDOW], 0.0)
+            lev1.append(window)
+        nc.gpsimd.memset(w2s[:].bitcast(I32), 0)
+        nc.gpsimd.dma_start(unit_sb[:], unit.rearrange("(p t) o -> p (t o)", t=PACK))
+        nc.gpsimd.dma_start(w2w[:].bitcast(I32), w2_words[0].bitcast(I32))
+        for j in range(4):
+            nc.gpsimd.dma_start(w2s[j:P:32, :].bitcast(I32), w2_scales[0, j:SCALE_ROWS:4, :].bitcast(I32))
+
+        nc.scalar.copy(
+            w1w[:].bitcast(U16).rearrange("p (t m) -> p t m", t=PACK),
+            w1w_raw[:].bitcast(U16).rearrange("p (m t) -> p t m", t=PACK),
+        )
+
+        nc.vector.tensor_copy(xs_picked[:], xs[:].indirect(offs_sb[:]))
+        for q in range(4):
+            nc.scalar.dma_start(
+                xs_placed[32 * q : 32 * q + 4, :].bitcast(I32),
+                xs_picked[PARK + 4 * q : PARK + 4 * q + 4, :].bitcast(I32),
+            )
+        lod_sb = keep.tile([P, PACK, U], F32, name="lod_sb", tag="picked_then_lod", align_bytes=64)
+        nc.sync.dma_start(lod_sb[:], lod.rearrange("(p t) r -> p t r", t=PACK))
+        nc.vector.tensor_copy(
+            w1s[:].rearrange("p (t m) -> p t m", t=PACK),
+            w1s_raw[:].rearrange("p (m t) -> p t m", t=PACK),
+        )
+
+        y = {}
+        for h in range(S // HALF):
+            picked = keep.tile([P, HALF], U32, name="picked_%d" % h, align_bytes=64)
+            nc.vector.tensor_copy(picked[:], xw[:].indirect(offs_sb[:, h * HALF // 16 : (h + 1) * HALF // 16]))
+            for t in range(PACK):
+                bank = psum.tile([P, HALF], F32, name="bank_%d" % (2 * t + h))
+                nc.tensor.matmul_mx(
+                    out=bank[:],
+                    lhsT=w1w[:, 2 * P * t : 2 * P * (t + 1)].bitcast(FP4X4),
+                    lhsT_scale=w1s[:, P * t : P * (t + 1)],
+                    rhs=picked[:].bitcast(FP8X4),
+                    rhs_scale=xs_placed[:, h * HALF : (h + 1) * HALF],
+                    start=True,
+                    stop=True,
+                )
+                y[t, h] = bank
+
+        lp = []
+        for t in range(PACK):
+            for h in range(S // HALF):
+                nc.vector.tensor_reduce(
+                    lev1[t][:, h * HALF // D : (h + 1) * HALF // D],
+                    y[t, h][:].rearrange("p (v d) -> p v d", d=D),
+                    AXIS.X,
+                    ALU.max,
+                )
+            looked = keep.tile([P, U], F32, name="lp_%d" % t)
+            if t < PACK - 1:
+                nc.scalar.activation(looked[:], lev1[t][:].indirect(par_sb[:]), ACT.Copy)
+            else:
+                nc.vector.tensor_copy(looked[:], lev1[t][:].indirect(par_sb[:]))
+            lp.append(looked)
+        lev2 = []
+        for t in range(PACK):
+            level = keep.tile([P, U], F32, name="lev2_%d" % t)
+            nc.vector.scalar_tensor_tensor(level[:], lod_sb[:, t, :], 0.7, lp[t][:], ALU.mult, ALU.add)
+            lev2.append(level)
+
+        for c, (r0, r1) in enumerate(CHUNKS):
+            width = r1 - r0
+            planes = keep.tile([P, PACK, width], BF16, name="planes_%d" % c, align_bytes=64)
+            for t in range(PACK):
+                near = keep.tile([P, width], F32, name="near_%d_%d" % (c, t))
+                diff = keep.tile([P, width], F32, name="diff_%d_%d" % (c, t))
+                both = keep.tile([P, width], F32, name="both_%d_%d" % (c, t))
+                bent = keep.tile([P, width], F32, name="bent_%d_%d" % (c, t))
+                gate = keep.tile([P, width], F32, name="gate_%d_%d" % (c, t))
+                nc.scalar.activation(near[:], lev2[t][:].indirect(nb_sb[:, r0 // 16 : r1 // 16]), ACT.Copy)
+                nc.vector.tensor_tensor(diff[:], lev2[t][:, r0:r1], near[:], ALU.subtract)
+                nc.vector.tensor_tensor(both[:], lev2[t][:, r0:r1], near[:], ALU.add)
+                nc.scalar.activation(bent[:], diff[:], ACT.Tanh, scale=0.5)
+                nc.scalar.activation(gate[:], bent[:], ACT.Exp, scale=0.8, bias=math.log(0.5))
+                nc.vector.scalar_tensor_tensor(
+                    planes[:, t, :], both[:], unit_sb[:, t : t + 1], gate[:], ALU.mult, ALU.mult
+                )
+            woven = keep.tile([P, width, PACK], BF16, name="woven_%d" % c, align_bytes=64)
+            nc.vector.tensor_copy(
+                woven[:].rearrange("p (a i) t -> p a t i", i=4),
+                planes[:].rearrange("p t (a i) -> p a t i", i=4),
+            )
+            codes = keep.tile([P, width], U32, name="codes_%d" % c, align_bytes=64)
+            scales = keep.tile([P, width], U8, name="scales_%d" % c, align_bytes=64)
+            nc.vector.quantize_mx(
+                out=codes[:].bitcast(FP8X4), scales=scales[:], in_=woven[:].rearrange("p r t -> p (r t)")
+            )
+            for m in range(N // P):
+                acc = psum.tile([P, width], F32, name="bank_%d" % (2 * c + m))
+                nc.tensor.matmul_mx(
+                    out=acc[:],
+                    lhsT=w2w[:, 2 * P * m : 2 * P * (m + 1)].bitcast(FP4X4),
+                    lhsT_scale=w2s[:, P * m : P * (m + 1)],
+                    rhs=codes[:].bitcast(FP8X4),
+                    rhs_scale=scales[:],
+                    start=True,
+                    stop=True,
+                )
+                result = keep.tile([P, width], F32, name="result_%d_%d" % (c, m))
+                if m == 0:
+                    nc.scalar.copy(result[:], acc[:])
+                else:
+                    nc.vector.tensor_copy(result[:], acc[:])
+                nc.sync.dma_start(out[P * m : P * (m + 1), r0:r1], result[:])

@@ -1,4 +1,3 @@
-import math
 from contextlib import ExitStack
 
 import concourse.mybir as mybir
@@ -23,8 +22,9 @@ PACK = 4
 HALF = 512
 SCALE_ROWS = 16
 PARK = P - SCALE_ROWS
-LEV1_WINDOW = 704
-CHUNKS = ((0, 256), (256, 512))
+SCALAR_WINDOW = U + 16
+VECTOR_WINDOW = 704
+CHUNKS = ((0, 256), (256, 384), (384, 512))
 
 
 def tile_picked_yoctree_exp_p_kernel(
@@ -49,6 +49,9 @@ def tile_picked_yoctree_exp_p_kernel(
         w2w = keep.tile([P, 2 * N], U8, name="w2w", align_bytes=64)
         w2s = keep.tile([P, N], U8, name="w2s", align_bytes=64)
         unit_sb = keep.tile([P, PACK], F32, name="unit_sb")
+        half_unit = keep.tile([P, PACK], F32, name="half_unit")
+        safe_unit = keep.tile([P, PACK], F32, name="safe_unit")
+        inv_unit = keep.tile([P, PACK], F32, name="inv_unit")
         xs_picked = keep.tile([P, S], U8, name="xs_picked", tag="picked_then_lod", align_bytes=64)
         xs_placed = keep.tile([P, S], U8, name="xs_placed", align_bytes=64)
 
@@ -56,6 +59,7 @@ def tile_picked_yoctree_exp_p_kernel(
         nc.scalar.dma_start(xs[PARK:P, :].bitcast(I32), x_scales[0].bitcast(I32))
         nc.sync.dma_start(par_sb[:], par)
         nc.scalar.dma_start(w1w_raw[:].bitcast(I32), w1_words[0].bitcast(I32))
+        nc.scalar.dma_start(unit_sb[:], unit.rearrange("(p t) o -> p (t o)", t=PACK))
         nc.sync.dma_start(xw[:].bitcast(I32), x_words[0].rearrange("p n t -> p (n t)").bitcast(I32))
         nc.sync.dma_start(nb_sb[:], nb)
 
@@ -65,13 +69,16 @@ def tile_picked_yoctree_exp_p_kernel(
         for j in range(4):
             queue = nc.scalar if j < 2 else nc.gpsimd
             queue.dma_start(w1s_raw[j:P:32, :].bitcast(I32), w1_scales[0, j:SCALE_ROWS:4, :].bitcast(I32))
-        lev1 = []
+        lev1, lev2 = [], []
         for t in range(PACK):
-            window = keep.tile([P, LEV1_WINDOW], F32, name="lev1_%d" % t)
-            nc.gpsimd.memset(window[:, V:LEV1_WINDOW], 0.0)
+            window = keep.tile([P, SCALAR_WINDOW], F32, name="lev1_%d" % t)
+            nc.gpsimd.memset(window[:, V:], 0.0)
             lev1.append(window)
+        for t in range(PACK):
+            window = keep.tile([P, VECTOR_WINDOW if t == 0 else SCALAR_WINDOW], F32, name="lev2_%d" % t)
+            nc.gpsimd.memset(window[:, U:], 0.0)
+            lev2.append(window)
         nc.gpsimd.memset(w2s[:].bitcast(I32), 0)
-        nc.gpsimd.dma_start(unit_sb[:], unit.rearrange("(p t) o -> p (t o)", t=PACK))
         nc.gpsimd.dma_start(w2w[:].bitcast(I32), w2_words[0].bitcast(I32))
         for j in range(4):
             nc.gpsimd.dma_start(w2s[j:P:32, :].bitcast(I32), w2_scales[0, j:SCALE_ROWS:4, :].bitcast(I32))
@@ -80,6 +87,7 @@ def tile_picked_yoctree_exp_p_kernel(
             w1w[:].bitcast(U16).rearrange("p (t m) -> p t m", t=PACK),
             w1w_raw[:].bitcast(U16).rearrange("p (m t) -> p t m", t=PACK),
         )
+        nc.scalar.activation(half_unit[:], unit_sb[:], ACT.Copy, scale=0.5)
 
         nc.vector.tensor_copy(xs_picked[:], xs[:].indirect(offs_sb[:]))
         for q in range(4):
@@ -88,81 +96,98 @@ def tile_picked_yoctree_exp_p_kernel(
                 xs_picked[PARK + 4 * q : PARK + 4 * q + 4, :].bitcast(I32),
             )
         lod_sb = keep.tile([P, PACK, U], F32, name="lod_sb", tag="picked_then_lod", align_bytes=64)
-        nc.sync.dma_start(lod_sb[:], lod.rearrange("(p t) r -> p t r", t=PACK))
+        lod_rows = lod.rearrange("(p t) r -> p t r", t=PACK)
+        own = []
+        for t in range(PACK):
+            nc.sync.dma_start(lod_sb[:, t, :], lod_rows[:, t, :])
+            scaled = keep.tile([P, U], F32, name="own_%d" % t)
+            nc.gpsimd.tensor_scalar(scaled[:], lod_sb[:, t, :], half_unit[:, t : t + 1], 0.7, ALU.mult, ALU.mult)
+            own.append(scaled)
         nc.vector.tensor_copy(
             w1s[:].rearrange("p (t m) -> p t m", t=PACK),
             w1s_raw[:].rearrange("p (m t) -> p t m", t=PACK),
         )
+        nc.vector.scalar_tensor_tensor(safe_unit[:], unit_sb[:], 0.0, unit_sb[:], ALU.is_equal, ALU.add)
+        nc.vector.reciprocal(inv_unit[:], safe_unit[:])
 
-        y = {}
+        picked = []
         for h in range(S // HALF):
-            picked = keep.tile([P, HALF], U32, name="picked_%d" % h, align_bytes=64)
-            nc.vector.tensor_copy(picked[:], xw[:].indirect(offs_sb[:, h * HALF // 16 : (h + 1) * HALF // 16]))
-            for t in range(PACK):
+            words = keep.tile([P, HALF], U32, name="picked_%d" % h, align_bytes=64)
+            nc.vector.tensor_copy(words[:], xw[:].indirect(offs_sb[:, h * HALF // 16 : (h + 1) * HALF // 16]))
+            picked.append(words)
+
+        lp = []
+        for t in range(PACK):
+            for h in range(S // HALF):
                 bank = psum.tile([P, HALF], F32, name="bank_%d" % (2 * t + h))
                 nc.tensor.matmul_mx(
                     out=bank[:],
                     lhsT=w1w[:, 2 * P * t : 2 * P * (t + 1)].bitcast(FP4X4),
                     lhsT_scale=w1s[:, P * t : P * (t + 1)],
-                    rhs=picked[:].bitcast(FP8X4),
+                    rhs=picked[h][:].bitcast(FP8X4),
                     rhs_scale=xs_placed[:, h * HALF : (h + 1) * HALF],
                     start=True,
                     stop=True,
                 )
-                y[t, h] = bank
-
-        lp = []
-        for t in range(PACK):
-            for h in range(S // HALF):
                 nc.vector.tensor_reduce(
                     lev1[t][:, h * HALF // D : (h + 1) * HALF // D],
-                    y[t, h][:].rearrange("p (v d) -> p v d", d=D),
+                    bank[:].rearrange("p (v d) -> p v d", d=D),
                     AXIS.X,
                     ALU.max,
                 )
             looked = keep.tile([P, U], F32, name="lp_%d" % t)
-            if t < PACK - 1:
-                nc.scalar.activation(looked[:], lev1[t][:].indirect(par_sb[:]), ACT.Copy)
-            else:
-                nc.vector.tensor_copy(looked[:], lev1[t][:].indirect(par_sb[:]))
+            nc.scalar.activation(looked[:], lev1[t][:].indirect(par_sb[:]), ACT.Copy)
             lp.append(looked)
-        lev2 = []
         for t in range(PACK):
-            level = keep.tile([P, U], F32, name="lev2_%d" % t)
-            nc.vector.scalar_tensor_tensor(level[:], lod_sb[:, t, :], 0.7, lp[t][:], ALU.mult, ALU.add)
-            lev2.append(level)
+            nc.vector.scalar_tensor_tensor(
+                lev2[t][:, 0:U], lp[t][:], half_unit[:, t : t + 1], own[t][:], ALU.mult, ALU.add
+            )
 
+        near, det = [], []
+        for t in range(PACK):
+            fetched = keep.tile([P, U], F32, name="near_%d" % t)
+            if t == 0:
+                nc.vector.tensor_copy(fetched[:], lev2[t][:].indirect(nb_sb[:]))
+            else:
+                nc.scalar.activation(fetched[:], lev2[t][:].indirect(nb_sb[:]), ACT.Copy)
+            diff = keep.tile([P, U], F32, name="det_%d" % t)
+            nc.vector.tensor_tensor(diff[:], lev2[t][:, 0:U], fetched[:], ALU.subtract)
+            near.append(fetched)
+            det.append(diff)
+        smo = keep.tile([P, PACK, U], F32, name="smo")
+        bent = keep.tile([P, PACK, U], F32, name="bent")
+        for t in range(PACK):
+            nc.vector.tensor_tensor(smo[:, t, :], lev2[t][:, 0:U], near[t][:], ALU.add)
+            nc.scalar.activation(bent[:, t, :], det[t][:], ACT.Tanh, scale=inv_unit[:, t : t + 1])
+
+        out_rows = out.rearrange("(m p) r -> p m r", p=P)
         for c, (r0, r1) in enumerate(CHUNKS):
             width = r1 - r0
-            planes = keep.tile([P, PACK, width], BF16, name="planes_%d" % c, align_bytes=64)
-            for t in range(PACK):
-                near = keep.tile([P, width], F32, name="near_%d_%d" % (c, t))
-                diff = keep.tile([P, width], F32, name="diff_%d_%d" % (c, t))
-                both = keep.tile([P, width], F32, name="both_%d_%d" % (c, t))
-                bent = keep.tile([P, width], F32, name="bent_%d_%d" % (c, t))
-                gate = keep.tile([P, width], F32, name="gate_%d_%d" % (c, t))
-                nc.scalar.activation(near[:], lev2[t][:].indirect(nb_sb[:, r0 // 16 : r1 // 16]), ACT.Copy)
-                nc.vector.tensor_tensor(diff[:], lev2[t][:, r0:r1], near[:], ALU.subtract)
-                nc.vector.tensor_tensor(both[:], lev2[t][:, r0:r1], near[:], ALU.add)
-                nc.scalar.activation(bent[:], diff[:], ACT.Tanh, scale=0.5)
-                nc.scalar.activation(gate[:], bent[:], ACT.Exp, scale=0.8, bias=math.log(0.5))
-                nc.vector.scalar_tensor_tensor(
-                    planes[:, t, :], both[:], unit_sb[:, t : t + 1], gate[:], ALU.mult, ALU.mult
-                )
+            last = c == len(CHUNKS) - 1
+            gate = keep.tile([P, PACK, width], F32, name="gate_%d" % c)
+            nc.scalar.activation(gate[:], bent[:, :, r0:r1], ACT.Exp, scale=0.8)
             woven = keep.tile([P, width, PACK], BF16, name="woven_%d" % c, align_bytes=64)
-            nc.vector.tensor_copy(
+            nc.vector.tensor_tensor(
                 woven[:].rearrange("p (a i) t -> p a t i", i=4),
-                planes[:].rearrange("p t (a i) -> p a t i", i=4),
+                smo[:, :, r0:r1].rearrange("p t (a i) -> p a t i", i=4),
+                gate[:].rearrange("p t (a i) -> p a t i", i=4),
+                ALU.mult,
             )
             codes = keep.tile([P, width], U32, name="codes_%d" % c, align_bytes=64)
             scales = keep.tile([P, width], U8, name="scales_%d" % c, align_bytes=64)
             nc.vector.quantize_mx(
                 out=codes[:].bitcast(FP8X4), scales=scales[:], in_=woven[:].rearrange("p r t -> p (r t)")
             )
+            result = keep.tile([P, N // P, width], F32, name="result_%d" % c)
+            shared = psum.tile([P, N // P, width], F32, name="bank_%d" % c)
             for m in range(N // P):
-                acc = psum.tile([P, width], F32, name="bank_%d" % (2 * c + m))
+                if last and m == 1:
+                    spare = psum.tile([P, width], F32, name="bank_%d" % (c + 1))
+                    acc = spare[:]
+                else:
+                    acc = shared[:, m, :]
                 nc.tensor.matmul_mx(
-                    out=acc[:],
+                    out=acc,
                     lhsT=w2w[:, 2 * P * m : 2 * P * (m + 1)].bitcast(FP4X4),
                     lhsT_scale=w2s[:, P * m : P * (m + 1)],
                     rhs=codes[:].bitcast(FP8X4),
@@ -170,9 +195,10 @@ def tile_picked_yoctree_exp_p_kernel(
                     start=True,
                     stop=True,
                 )
-                result = keep.tile([P, width], F32, name="result_%d_%d" % (c, m))
-                if m == 0:
-                    nc.scalar.copy(result[:], acc[:])
-                else:
-                    nc.vector.tensor_copy(result[:], acc[:])
-                nc.sync.dma_start(out[P * m : P * (m + 1), r0:r1], result[:])
+                if last and m == 0:
+                    nc.scalar.copy(result[:, m, :], acc)
+                if last and m == 1:
+                    nc.vector.tensor_copy(result[:, m, :], acc)
+            if not last:
+                nc.scalar.copy(result[:], shared[:])
+            nc.sync.dma_start(out_rows[:, :, r0:r1], result[:])

@@ -24,6 +24,7 @@ SCALE_ROWS = 16
 PARK = P - SCALE_ROWS
 SCALAR_WINDOW = U + 16
 VECTOR_WINDOW = 704
+PIECES = (((0, 512),), ((0, 256), (256, 512)))
 CHUNKS = ((0, 256), (256, 384), (384, 512))
 
 
@@ -41,34 +42,43 @@ def tile_picked_yoctree_exp_p_kernel(
         nb_sb = lists.tile([P, U // 16], U16, name="nb_sb")
 
         xw = keep.tile([P, T], U32, name="xw", align_bytes=64)
-        xs = keep.tile([P, T], U8, name="xs", align_bytes=64)
+        xs = keep.tile([P, T], U8, name="xs", tag="xs_then_lod", align_bytes=64)
         w1w_raw = keep.tile([P, 2 * H], U8, name="w1w_raw", align_bytes=64)
         w1s_raw = keep.tile([P, H], U8, name="w1s_raw", align_bytes=64)
+        w1s_dealt = keep.tile([P, H], U8, name="w1s_dealt", tag="w1s_then_w2w", align_bytes=64)
         w1w = keep.tile([P, 2 * H], U8, name="w1w", align_bytes=64)
         w1s = keep.tile([P, H], U8, name="w1s", align_bytes=64)
-        w2w = keep.tile([P, 2 * N], U8, name="w2w", align_bytes=64)
-        w2s = keep.tile([P, N], U8, name="w2s", align_bytes=64)
         unit_sb = keep.tile([P, PACK], F32, name="unit_sb")
         half_unit = keep.tile([P, PACK], F32, name="half_unit")
+        lod_unit = keep.tile([P, PACK], F32, name="lod_unit")
         safe_unit = keep.tile([P, PACK], F32, name="safe_unit")
         inv_unit = keep.tile([P, PACK], F32, name="inv_unit")
-        xs_picked = keep.tile([P, S], U8, name="xs_picked", tag="picked_then_lod", align_bytes=64)
+        xs_picked = keep.tile([P, S], U8, name="xs_picked", tag="picked_then_w2s", align_bytes=64)
         xs_placed = keep.tile([P, S], U8, name="xs_placed", align_bytes=64)
 
         nc.sync.dma_start(offs_sb[:], offs)
         nc.scalar.dma_start(xs[PARK:P, :].bitcast(I32), x_scales[0].bitcast(I32))
+        nc.sync.dma_start(w1s_raw[PARK:P, :].bitcast(I32), w1_scales[0].bitcast(I32))
+        nc.scalar.dma_start(unit_sb[:], unit.rearrange("(p t) o -> p (t o)", t=PACK))
         nc.sync.dma_start(par_sb[:], par)
         nc.scalar.dma_start(w1w_raw[:].bitcast(I32), w1_words[0].bitcast(I32))
-        nc.scalar.dma_start(unit_sb[:], unit.rearrange("(p t) o -> p (t o)", t=PACK))
         nc.sync.dma_start(xw[:].bitcast(I32), x_words[0].rearrange("p n t -> p (n t)").bitcast(I32))
         nc.sync.dma_start(nb_sb[:], nb)
 
         nc.vector.memset(xs[0:PARK, :].bitcast(I32), 0)
         nc.vector.memset(xs_placed[:].bitcast(I32), 0)
-        nc.gpsimd.memset(w1s_raw[:].bitcast(I32), 0)
-        for j in range(4):
-            queue = nc.scalar if j < 2 else nc.gpsimd
-            queue.dma_start(w1s_raw[j:P:32, :].bitcast(I32), w1_scales[0, j:SCALE_ROWS:4, :].bitcast(I32))
+        nc.gpsimd.memset(w1s_raw[0:PARK, :].bitcast(I32), 0)
+        nc.gpsimd.memset(w1s[:].bitcast(I32), 0)
+        nc.vector.tensor_copy(
+            w1s_dealt[:].rearrange("p (t m) -> p t m", t=PACK),
+            w1s_raw[:].rearrange("p (m t) -> p t m", t=PACK),
+        )
+        for q in range(4):
+            queue = nc.sync if q < 2 else nc.gpsimd
+            queue.dma_start(
+                w1s[32 * q : 32 * q + 4, :].bitcast(I32),
+                w1s_dealt[PARK + 4 * q : PARK + 4 * q + 4, :].bitcast(I32),
+            )
         lev1, lev2 = [], []
         for t in range(PACK):
             window = keep.tile([P, SCALAR_WINDOW], F32, name="lev1_%d" % t)
@@ -78,57 +88,59 @@ def tile_picked_yoctree_exp_p_kernel(
             window = keep.tile([P, VECTOR_WINDOW if t == 0 else SCALAR_WINDOW], F32, name="lev2_%d" % t)
             nc.gpsimd.memset(window[:, U:], 0.0)
             lev2.append(window)
-        nc.gpsimd.memset(w2s[:].bitcast(I32), 0)
-        nc.gpsimd.dma_start(w2w[:].bitcast(I32), w2_words[0].bitcast(I32))
-        for j in range(4):
-            nc.gpsimd.dma_start(w2s[j:P:32, :].bitcast(I32), w2_scales[0, j:SCALE_ROWS:4, :].bitcast(I32))
 
         nc.scalar.copy(
             w1w[:].bitcast(U16).rearrange("p (t m) -> p t m", t=PACK),
             w1w_raw[:].bitcast(U16).rearrange("p (m t) -> p t m", t=PACK),
         )
         nc.scalar.activation(half_unit[:], unit_sb[:], ACT.Copy, scale=0.5)
+        nc.scalar.activation(lod_unit[:], unit_sb[:], ACT.Copy, scale=0.5 * 0.7)
 
         nc.vector.tensor_copy(xs_picked[:], xs[:].indirect(offs_sb[:]))
         for q in range(4):
-            nc.scalar.dma_start(
+            nc.sync.dma_start(
                 xs_placed[32 * q : 32 * q + 4, :].bitcast(I32),
                 xs_picked[PARK + 4 * q : PARK + 4 * q + 4, :].bitcast(I32),
             )
-        lod_sb = keep.tile([P, PACK, U], F32, name="lod_sb", tag="picked_then_lod", align_bytes=64)
+        lod_sb = keep.tile([P, PACK, U], F32, name="lod_sb", tag="xs_then_lod", align_bytes=64)
         lod_rows = lod.rearrange("(p t) r -> p t r", t=PACK)
         own = []
         for t in range(PACK):
             nc.sync.dma_start(lod_sb[:, t, :], lod_rows[:, t, :])
             scaled = keep.tile([P, U], F32, name="own_%d" % t)
-            nc.gpsimd.tensor_scalar(scaled[:], lod_sb[:, t, :], half_unit[:, t : t + 1], 0.7, ALU.mult, ALU.mult)
+            nc.gpsimd.tensor_scalar(scaled[:], lod_sb[:, t, :], lod_unit[:, t : t + 1], 0.0, ALU.mult, ALU.add)
             own.append(scaled)
-        nc.vector.tensor_copy(
-            w1s[:].rearrange("p (t m) -> p t m", t=PACK),
-            w1s_raw[:].rearrange("p (m t) -> p t m", t=PACK),
-        )
+        w2w = keep.tile([P, 2 * N], U8, name="w2w", tag="w1s_then_w2w", align_bytes=64)
+        nc.sync.dma_start(w2w[:].bitcast(I32), w2_words[0].bitcast(I32))
+        w2s = keep.tile([P, N], U8, name="w2s", tag="picked_then_w2s", align_bytes=64)
+        nc.gpsimd.memset(w2s[:].bitcast(I32), 0)
+        for j in range(4):
+            nc.sync.dma_start(w2s[j:P:32, :].bitcast(I32), w2_scales[0, j:SCALE_ROWS:4, :].bitcast(I32))
         nc.vector.scalar_tensor_tensor(safe_unit[:], unit_sb[:], 0.0, unit_sb[:], ALU.is_equal, ALU.add)
         nc.vector.reciprocal(inv_unit[:], safe_unit[:])
 
         picked = []
         for h in range(S // HALF):
             words = keep.tile([P, HALF], U32, name="picked_%d" % h, align_bytes=64)
-            nc.vector.tensor_copy(words[:], xw[:].indirect(offs_sb[:, h * HALF // 16 : (h + 1) * HALF // 16]))
+            for j0, j1 in PIECES[h]:
+                first = h * HALF
+                nc.vector.tensor_copy(words[:, j0:j1], xw[:].indirect(offs_sb[:, (first + j0) // 16 : (first + j1) // 16]))
             picked.append(words)
 
         lp = []
         for t in range(PACK):
             for h in range(S // HALF):
                 bank = psum.tile([P, HALF], F32, name="bank_%d" % (2 * t + h))
-                nc.tensor.matmul_mx(
-                    out=bank[:],
-                    lhsT=w1w[:, 2 * P * t : 2 * P * (t + 1)].bitcast(FP4X4),
-                    lhsT_scale=w1s[:, P * t : P * (t + 1)],
-                    rhs=picked[h][:].bitcast(FP8X4),
-                    rhs_scale=xs_placed[:, h * HALF : (h + 1) * HALF],
-                    start=True,
-                    stop=True,
-                )
+                for j0, j1 in PIECES[h] if t == 0 else ((0, HALF),):
+                    nc.tensor.matmul_mx(
+                        out=bank[:, j0:j1],
+                        lhsT=w1w[:, 2 * P * t : 2 * P * (t + 1)].bitcast(FP4X4),
+                        lhsT_scale=w1s[:, P * t : P * (t + 1)],
+                        rhs=picked[h][:, j0:j1].bitcast(FP8X4),
+                        rhs_scale=xs_placed[:, h * HALF + j0 : h * HALF + j1],
+                        start=True,
+                        stop=True,
+                    )
                 nc.vector.tensor_reduce(
                     lev1[t][:, h * HALF // D : (h + 1) * HALF // D],
                     bank[:].rearrange("p (v d) -> p v d", d=D),
@@ -197,8 +209,10 @@ def tile_picked_yoctree_exp_p_kernel(
                 )
                 if last and m == 0:
                     nc.scalar.copy(result[:, m, :], acc)
+                    nc.scalar.dma_start(out_rows[:, m, r0:r1], result[:, m, :])
                 if last and m == 1:
                     nc.vector.tensor_copy(result[:, m, :], acc)
+                    nc.sync.dma_start(out_rows[:, m, r0:r1], result[:, m, :])
             if not last:
                 nc.scalar.copy(result[:], shared[:])
-            nc.sync.dma_start(out_rows[:, :, r0:r1], result[:])
+                nc.sync.dma_start(out_rows[:, :, r0:r1], result[:])

from contextlib import ExitStack

import concourse.mybir as mybir

K, T, S, D, N, H, V, U = 512, 4096, 1024, 4, 256, 512, 256, 512
FLOPS = 2 * K * H * S + 2 * H * N * U

F32 = mybir.dt.float32
BF16 = mybir.dt.bfloat16
I32 = mybir.dt.int32
U32 = mybir.dt.uint32
U16 = mybir.dt.uint16
U8 = mybir.dt.uint8
FP8X4 = mybir.dt.float8_e4m3fn_x4
FP4X4 = mybir.dt.float4_e2m1fn_x4
ALU = mybir.AluOpType
ACT = mybir.ActivationFunctionType
AXIS = mybir.AxisListType

P = 128
PACK = 4
HALF = 512
SCALE_ROWS = 16
PARK = P - SCALE_ROWS
SCALAR_WINDOW = U + 16
VECTOR_WINDOW = 704
PIECES = (((0, 512),), ((0, 256), (256, 512)))
CHUNKS = ((0, 256), (256, 384), (384, 512))


def tile_picked_yoctree_exp_p_kernel(
    tc, x_words, x_scales, w1_words, w1_scales, lod, unit, w2_words, w2_scales, offs, par, nb, out
):
    nc = tc.nc
    with ExitStack() as ctx:
        lists = ctx.enter_context(tc.tile_pool(name="lists", bufs=1))
        keep = ctx.enter_context(tc.tile_pool(name="keep", bufs=1))
        psum = ctx.enter_context(tc.psum_pool(name="psum", bufs=1))

        offs_sb = lists.tile([P, S // 16], U16, name="offs_sb")
        par_sb = lists.tile([P, U // 16], U16, name="par_sb")
        nb_sb = lists.tile([P, U // 16], U16, name="nb_sb")

        xw = keep.tile([P, T], U32, name="xw", align_bytes=64)
        xs = keep.tile([P, T], U8, name="xs", tag="xs_then_lod", align_bytes=64)
        w1w_raw = keep.tile([P, 2 * H], U8, name="w1w_raw", align_bytes=64)
        w1s_raw = keep.tile([P, H], U8, name="w1s_raw", align_bytes=64)
        w1s_dealt = keep.tile([P, H], U8, name="w1s_dealt", tag="w1s_then_w2w", align_bytes=64)
        w1w = keep.tile([P, 2 * H], U8, name="w1w", align_bytes=64)
        w1s = keep.tile([P, H], U8, name="w1s", align_bytes=64)
        unit_sb = keep.tile([P, PACK], F32, name="unit_sb")
        half_unit = keep.tile([P, PACK], F32, name="half_unit")
        lod_unit = keep.tile([P, PACK], F32, name="lod_unit")
        safe_unit = keep.tile([P, PACK], F32, name="safe_unit")
        inv_unit = keep.tile([P, PACK], F32, name="inv_unit")
        xs_picked = keep.tile([P, S], U8, name="xs_picked", tag="picked_then_w2s", align_bytes=64)
        xs_placed = keep.tile([P, S], U8, name="xs_placed", align_bytes=64)

        nc.sync.dma_start(offs_sb[:], offs)
        nc.scalar.dma_start(xs[PARK:P, :].bitcast(I32), x_scales[0].bitcast(I32))
        nc.sync.dma_start(w1s_raw[PARK:P, :].bitcast(I32), w1_scales[0].bitcast(I32))
        nc.scalar.dma_start(unit_sb[:], unit.rearrange("(p t) o -> p (t o)", t=PACK))
        nc.sync.dma_start(par_sb[:], par)
        nc.scalar.dma_start(w1w_raw[:].bitcast(I32), w1_words[0].bitcast(I32))
        nc.sync.dma_start(xw[:].bitcast(I32), x_words[0].rearrange("p n t -> p (n t)").bitcast(I32))
        nc.sync.dma_start(nb_sb[:], nb)

        nc.vector.memset(xs[0:PARK, :].bitcast(I32), 0)
        nc.vector.memset(xs_placed[:].bitcast(I32), 0)
        nc.gpsimd.memset(w1s_raw[0:PARK, :].bitcast(I32), 0)
        nc.gpsimd.memset(w1s[:].bitcast(I32), 0)
        nc.vector.tensor_copy(
            w1s_dealt[:].rearrange("p (t m) -> p t m", t=PACK),
            w1s_raw[:].rearrange("p (m t) -> p t m", t=PACK),
        )
        for q in range(4):
            queue = nc.sync if q < 2 else nc.gpsimd
            queue.dma_start(
                w1s[32 * q : 32 * q + 4, :].bitcast(I32),
                w1s_dealt[PARK + 4 * q : PARK + 4 * q + 4, :].bitcast(I32),
            )
        lev1, lev2 = [], []
        for t in range(PACK):
            window = keep.tile([P, SCALAR_WINDOW], F32, name="lev1_%d" % t)
            nc.gpsimd.memset(window[:, V:], 0.0)
            lev1.append(window)
        for t in range(PACK):
            window = keep.tile([P, VECTOR_WINDOW if t == 0 else SCALAR_WINDOW], F32, name="lev2_%d" % t)
            nc.gpsimd.memset(window[:, U:], 0.0)
            lev2.append(window)

        nc.scalar.copy(
            w1w[:].bitcast(U16).rearrange("p (t m) -> p t m", t=PACK),
            w1w_raw[:].bitcast(U16).rearrange("p (m t) -> p t m", t=PACK),
        )
        nc.scalar.activation(half_unit[:], unit_sb[:], ACT.Copy, scale=0.5)
        nc.scalar.activation(lod_unit[:], unit_sb[:], ACT.Copy, scale=0.5 * 0.7)

        nc.vector.tensor_copy(xs_picked[:], xs[:].indirect(offs_sb[:]))
        for q in range(4):
            nc.sync.dma_start(
                xs_placed[32 * q : 32 * q + 4, :].bitcast(I32),
                xs_picked[PARK + 4 * q : PARK + 4 * q + 4, :].bitcast(I32),
            )
        lod_sb = keep.tile([P, PACK, U], F32, name="lod_sb", tag="xs_then_lod", align_bytes=64)
        lod_rows = lod.rearrange("(p t) r -> p t r", t=PACK)
        own = []
        for t in range(PACK):
            nc.sync.dma_start(lod_sb[:, t, :], lod_rows[:, t, :])
            scaled = keep.tile([P, U], F32, name="own_%d" % t)
            nc.gpsimd.tensor_scalar(scaled[:], lod_sb[:, t, :], lod_unit[:, t : t + 1], 0.0, ALU.mult, ALU.add)
            own.append(scaled)
        w2w = keep.tile([P, 2 * N], U8, name="w2w", tag="w1s_then_w2w", align_bytes=64)
        nc.sync.dma_start(w2w[:].bitcast(I32), w2_words[0].bitcast(I32))
        w2s = keep.tile([P, N], U8, name="w2s", tag="picked_then_w2s", align_bytes=64)
        nc.gpsimd.memset(w2s[:].bitcast(I32), 0)
        for j in range(4):
            nc.sync.dma_start(w2s[j:P:32, :].bitcast(I32), w2_scales[0, j:SCALE_ROWS:4, :].bitcast(I32))
        nc.vector.scalar_tensor_tensor(safe_unit[:], unit_sb[:], 0.0, unit_sb[:], ALU.is_equal, ALU.add)
        nc.vector.reciprocal(inv_unit[:], safe_unit[:])

        picked = []
        for h in range(S // HALF):
            words = keep.tile([P, HALF], U32, name="picked_%d" % h, align_bytes=64)
            for j0, j1 in PIECES[h]:
                first = h * HALF
                nc.vector.tensor_copy(words[:, j0:j1], xw[:].indirect(offs_sb[:, (first + j0) // 16 : (first + j1) // 16]))
            picked.append(words)

        lp = []
        for t in range(PACK):
            for h in range(S // HALF):
                bank = psum.tile([P, HALF], F32, name="bank_%d" % (2 * t + h))
                for j0, j1 in PIECES[h] if t == 0 else ((0, HALF),):
                    nc.tensor.matmul_mx(
                        out=bank[:, j0:j1],
                        lhsT=w1w[:, 2 * P * t : 2 * P * (t + 1)].bitcast(FP4X4),
                        lhsT_scale=w1s[:, P * t : P * (t + 1)],
                        rhs=picked[h][:, j0:j1].bitcast(FP8X4),
                        rhs_scale=xs_placed[:, h * HALF + j0 : h * HALF + j1],
                        start=True,
                        stop=True,
                    )
                nc.vector.tensor_reduce(
                    lev1[t][:, h * HALF // D : (h + 1) * HALF // D],
                    bank[:].rearrange("p (v d) -> p v d", d=D),
                    AXIS.X,
                    ALU.max,
                )
            looked = keep.tile([P, U], F32, name="lp_%d" % t)
            nc.scalar.activation(looked[:], lev1[t][:].indirect(par_sb[:]), ACT.Copy)
            lp.append(looked)
        for t in range(PACK):
            nc.vector.scalar_tensor_tensor(
                lev2[t][:, 0:U], lp[t][:], half_unit[:, t : t + 1], own[t][:], ALU.mult, ALU.add
            )

        near, det = [], []
        for t in range(PACK):
            fetched = keep.tile([P, U], F32, name="near_%d" % t)
            if t == 0:
                nc.vector.tensor_copy(fetched[:], lev2[t][:].indirect(nb_sb[:]))
            else:
                nc.scalar.activation(fetched[:], lev2[t][:].indirect(nb_sb[:]), ACT.Copy)
            diff = keep.tile([P, U], F32, name="det_%d" % t)
            nc.vector.tensor_tensor(diff[:], lev2[t][:, 0:U], fetched[:], ALU.subtract)
            near.append(fetched)
            det.append(diff)
        smo = keep.tile([P, PACK, U], F32, name="smo")
        bent = keep.tile([P, PACK, U], F32, name="bent")
        for t in range(PACK):
            nc.vector.tensor_tensor(smo[:, t, :], lev2[t][:, 0:U], near[t][:], ALU.add)
            nc.scalar.activation(bent[:, t, :], det[t][:], ACT.Tanh, scale=inv_unit[:, t : t + 1])

        out_rows = out.rearrange("(m p) r -> p m r", p=P)
        for c, (r0, r1) in enumerate(CHUNKS):
            width = r1 - r0
            last = c == len(CHUNKS) - 1
            gate = keep.tile([P, PACK, width], F32, name="gate_%d" % c)
            nc.scalar.activation(gate[:], bent[:, :, r0:r1], ACT.Exp, scale=0.8)
            woven = keep.tile([P, width, PACK], BF16, name="woven_%d" % c, align_bytes=64)
            nc.vector.tensor_tensor(
                woven[:].rearrange("p (a i) t -> p a t i", i=4),
                smo[:, :, r0:r1].rearrange("p t (a i) -> p a t i", i=4),
                gate[:].rearrange("p t (a i) -> p a t i", i=4),
                ALU.mult,
            )
            codes = keep.tile([P, width], U32, name="codes_%d" % c, align_bytes=64)
            scales = keep.tile([P, width], U8, name="scales_%d" % c, align_bytes=64)
            nc.vector.quantize_mx(
                out=codes[:].bitcast(FP8X4), scales=scales[:], in_=woven[:].rearrange("p r t -> p (r t)")
            )
            result = keep.tile([P, N // P, width], F32, name="result_%d" % c)
            shared = psum.tile([P, N // P, width], F32, name="bank_%d" % c)
            for m in range(N // P):
                if last and m == 1:
                    spare = psum.tile([P, width], F32, name="bank_%d" % (c + 1))
                    acc = spare[:]
                else:
                    acc = shared[:, m, :]
                nc.tensor.matmul_mx(
                    out=acc,
                    lhsT=w2w[:, 2 * P * m : 2 * P * (m + 1)].bitcast(FP4X4),
                    lhsT_scale=w2s[:, P * m : P * (m + 1)],
                    rhs=codes[:].bitcast(FP8X4),
                    rhs_scale=scales[:],
                    start=True,
                    stop=True,
                )
                if last and m == 0:
                    nc.scalar.copy(result[:, m, :], acc)
                    nc.scalar.dma_start(out_rows[:, m, r0:r1], result[:, m, :])
                if last and m == 1:
                    nc.vector.tensor_copy(result[:, m, :], acc)
                    nc.sync.dma_start(out_rows[:, m, r0:r1], result[:, m, :])
            if not last:
                nc.scalar.copy(result[:], shared[:])
                nc.sync.dma_start(out_rows[:, :, r0:r1], result[:])
